import numpy as np
import ml_dtypes


def mxq(x, axis, fmt="e4m3"):
    dtype, down = {"e4m3": (ml_dtypes.float8_e4m3fn, 7), "e5m2": (ml_dtypes.float8_e5m2, 14)}[fmt]
    v = np.moveaxis(np.asarray(x, np.float32).astype(ml_dtypes.bfloat16).astype(np.float64), axis, -1)
    blocks = v.reshape(v.shape[:-1] + (-1, 32))
    amax = np.abs(blocks).max(-1, keepdims=True)
    byte = np.maximum(np.where(amax > 0, np.frexp(amax)[1] - 1 + 127, 0) - down, 1)
    scale = np.exp2(byte - 127.0)
    codes = (blocks / scale).astype(np.float32).astype(dtype).astype(np.float64)
    return np.moveaxis((codes * scale).reshape(v.shape), -1, axis)


WIDE = False


def mx_kscale(k):
    if not WIDE:
        return np.ones(k)
    levels = np.array([10, -10, 5, -5, 0])
    if k % 512:
        return np.exp2(np.random.permutation(np.resize(levels, k // 32))).repeat(32)
    a = np.empty((k // 512, 16))
    for p in range(k // 512):
        a[p, :8] = np.random.permutation(np.resize(levels, 8))
        for g in range(8):
            far = levels[np.abs(levels - a[p, g]) >= 10]
            a[p, g + 8] = far[np.random.randint(len(far))]
    return np.exp2(a.ravel()).repeat(32)


def f64(x):
    return np.asarray(x).astype(np.float64)


def striped(idx):
    return np.tile(idx.reshape(-1, 16).T, (8, 1)).astype(np.uint16)


def unstriped(offs):
    return offs[:16].T.reshape(-1).astype(np.int64)


E2M1 = np.array([0.0, 0.5, 1.0, 1.5, 2.0, 3.0, 4.0, 6.0, -0.0, -0.5, -1.0, -1.5, -2.0, -3.0, -4.0, -6.0])


def pack_weight(w, fmt):
    k, n = w.shape
    w = f64(np.asarray(w, np.float32).astype(ml_dtypes.bfloat16)).reshape(k // 32, 32, n)
    amax = np.abs(w).max(1)
    if fmt == "e4m3":
        byte = np.frexp(amax)[1] - 1 + 127 - 7
    else:
        mant, ex = np.frexp(amax / 6.0)
        byte = np.where(mant > 0.5, ex, ex - 1) + 127
    byte = np.clip(np.where(amax > 0, byte, 1), 1, 254)
    scaled = (w * np.exp2(127.0 - byte)[:, None, :]).reshape(k, n).astype(np.float32)
    by_word = np.ascontiguousarray(scaled.reshape(k // 512, 128, 4, n).transpose(0, 1, 3, 2))
    if fmt == "e4m3":
        words = by_word.astype(ml_dtypes.float8_e4m3fn).view(np.uint8)
    else:
        c = by_word.astype(ml_dtypes.float4_e2m1fn).view(np.uint8) & 0xF
        words = (c[..., 0::2] | (c[..., 1::2] << 4)).reshape(k // 512, 128, 2 * n)
    return np.ascontiguousarray(words), np.ascontiguousarray(byte.astype(np.uint8).reshape(k // 512, 16, n))


def unpack_weight(words, scales, fmt):
    g, _, n = scales.shape
    words = np.ascontiguousarray(words).reshape(g, 128, n, -1)
    if fmt == "e4m3":
        vals = words.view(ml_dtypes.float8_e4m3fn).astype(np.float64)
    else:
        nib = np.empty((g, 128, n, 4), np.uint8)
        nib[..., 0::2] = words & 0xF
        nib[..., 1::2] = words >> 4
        vals = E2M1[nib]
    vals = vals * np.repeat(np.exp2(scales.astype(np.float64) - 127.0), 8, axis=1)[..., None]
    return vals.transpose(0, 1, 3, 2).reshape(g * 512, n)


def gelu(v):
    return 0.5 * v * (1.0 + np.tanh(np.sqrt(2.0 / np.pi) * (v + 0.044715 * v**3)))


K, H, T, S, T3, S2, P = 1024, 512, 4096, 1024, 2048, 1024, 512


def setup_inputs():
    n = np.random.standard_normal
    s = mx_kscale(K)[:, None]
    u = mx_kscale(H)[:, None]
    tab_words, tab_scales = pack_weight(n((K, T)) * s, "e4m3")
    tab2_words, tab2_scales = pack_weight(n((H, T3)) / np.sqrt(H) / u, "e4m3")
    w1_words, w1_scales = pack_weight(1.3 * n((K, H)) / np.sqrt(K) / s, "e2m1")
    w3_words, w3_scales = pack_weight(n((H, S2)) / np.sqrt(H) / u, "e4m3")
    return {
        "tab_words": tab_words, "tab_scales": tab_scales,
        "offs": striped(np.random.permutation(T)[:S]),
        "tab2_words": tab2_words, "tab2_scales": tab2_scales,
        "offs2": striped(np.random.permutation(T3)[:S2]),
        "pos1": striped(np.random.permutation(S)[:P]),
        "pos2": striped(np.random.permutation(S)[:P]),
        "w1_words": w1_words, "w1_scales": w1_scales,
        "w2": (0.55 * n((K, H)) / np.sqrt(K) / s).astype(np.float32),
        "w3_words": w3_words, "w3_scales": w3_scales,
        "gain1": (np.random.uniform(0.7, 2.0, H) * u[:, 0]).astype(np.float32),
        "gain2": (np.random.uniform(1.2, 3.0, H) * u[:, 0]).astype(np.float32),
        "margin": n(S2).astype(np.float32),
        "fit": (2.0 * n((S2, P))).astype(np.float32),
    }


def reference(tab_words, tab_scales, offs, tab2_words, tab2_scales, offs2, pos1, pos2,
              w1_words, w1_scales, w2, w3_words, w3_scales, gain1, gain2, margin, fit):
    v = unpack_weight(tab_words, tab_scales, "e4m3")[:, unstriped(offs)]
    v2 = unpack_weight(tab2_words, tab2_scales, "e4m3")[:, unstriped(offs2)]
    W1 = unpack_weight(w1_words, w1_scales, "e2m1")
    W3 = unpack_weight(w3_words, w3_scales, "e4m3")
    W2 = mxq(f64(w2), 0, "e4m3")
    h = f64(gain1)[:, None] * np.tanh(W1.T @ v)
    g = f64(gain2)[:, None] * np.sin(W2.T @ v)
    e = v2.T @ mxq(h, 0, "e4m3")
    d = W3.T @ mxq(g, 0, "e4m3")
    a = 1.0 / (1.0 + np.exp(-(e[:, unstriped(pos1)] + f64(margin)[:, None])))
    return np.maximum(a * f64(fit), d[:, unstriped(pos2)])

@@ -1,0 +1,236 @@
+import math
+from contextlib import ExitStack
+
+import concourse.mybir as mybir
+
+K, H, T, S, T3, S2, NP = 1024, 512, 4096, 1024, 2048, 1024, 512
+FLOPS = 2 * (2 * K * H * S + 2 * H * S2 * S)
+
+F32 = mybir.dt.float32
+BF16 = mybir.dt.bfloat16
+I32 = mybir.dt.int32
+U32 = mybir.dt.uint32
+U16 = mybir.dt.uint16
+U8 = mybir.dt.uint8
+FP8X4 = mybir.dt.float8_e4m3fn_x4
+FP4X4 = mybir.dt.float4_e2m1fn_x4
+ACT = mybir.ActivationFunctionType
+ALU = mybir.AluOpType
+
+P = 128
+PACK = 4
+QUADS = 4
+PASSES = K // (P * PACK)
+BANK = 512
+STRIP = BANK // PACK
+STRIPS = S // STRIP
+HALVES = S // BANK
+M_TILES = S2 // P
+V2_ROW = 8
+W3_ROW = 12
+E_ON_VECTOR = 5
+
+
+def tile_list_berth_filling_kernel(tc, tab_words, tab_scales, offs, tab2_words, tab2_scales, offs2,
+                                             pos1, pos2, w1_words, w1_scales, w2, w3_words, w3_scales,
+                                             gain1, gain2, margin, fit, out):
+    nc = tc.nc
+    with ExitStack() as ctx:
+        lists = ctx.enter_context(tc.tile_pool(name="lists", bufs=1))
+        keep = ctx.enter_context(tc.tile_pool(name="keep", bufs=1))
+        ring = ctx.enter_context(tc.tile_pool(name="ring", bufs=2))
+        psum = ctx.enter_context(tc.psum_pool(name="psum", bufs=8))
+
+        def words_of(dram):
+            return dram.rearrange("p n t -> p (n t)").bitcast(I32)
+
+        def load_list(dram, name):
+            tile = lists.tile(list(dram.shape), U16, name=name)
+            nc.sync.dma_start(tile[:], dram)
+            return tile
+
+        def zeroed_plane(shape, name, engine, tag=None):
+            tile = keep.tile(shape, U8, name=name, tag=tag or name, align_bytes=64)
+            engine.memset(tile[:].bitcast(I32), 0)
+            return tile
+
+        tab_sc = zeroed_plane([P, T], "tab_sc", nc.vector)
+        ones = ring.tile([P, 1], F32, name="ones", tag="big", align_bytes=64)
+        nc.vector.memset(ones[:], 1.0)
+        quarter_pi = keep.tile([P, 1], F32, name="quarter_pi")
+        nc.vector.tensor_scalar(quarter_pi[:], ones[:], math.pi / 4, None, ALU.mult)
+        w1_sc_raw = zeroed_plane([P, PASSES * H], "w1_sc_raw", nc.gpsimd, tag="w1_sc_raw")
+        for q in range(QUADS):
+            nc.gpsimd.dma_start(w1_sc_raw[32 * q:32 * q + 4, :].bitcast(I32).rearrange("r (a n) -> r a n", a=PASSES),
+                                w1_scales[:, 4 * q:4 * q + 4, :].bitcast(I32).rearrange("a r n -> r a n"))
+        v_sc1 = zeroed_plane([P, S], "v_sc1", nc.vector)
+        tab2_sc = zeroed_plane([P, T3], "tab2_sc", nc.vector)
+        w3_sc = zeroed_plane([P, S2], "w3_sc", nc.vector)
+        tab_w = [ring.tile([P, T], U32, name="tab_w", tag="big", align_bytes=64) for a in range(PASSES)]
+
+        idx = load_list(offs, "idx")
+        w1_raw = keep.tile([P, PASSES, 2 * H], U8, name="w1_raw")
+        nc.sync.dma_start(w1_raw[:].bitcast(I32), w1_words.rearrange("a p n -> p a n").bitcast(I32))
+        idx2 = load_list(offs2, "idx2")
+        nc.sync.dma_start(tab_w[0][:].bitcast(I32), words_of(tab_words[0]))
+        p1 = load_list(pos1, "p1")
+        p2 = load_list(pos2, "p2")
+        for q in range(QUADS):
+            nc.scalar.dma_start(tab_sc[32 * q:32 * q + 4 * PASSES, :].bitcast(I32),
+                                tab_scales[:, 4 * q:4 * q + 4, :].bitcast(I32))
+        nc.sync.dma_start(tab_w[1][:].bitcast(I32), words_of(tab_words[1]))
+
+        for q in range(QUADS):
+            nc.gpsimd.dma_start(tab2_sc[32 * q + V2_ROW:32 * q + V2_ROW + 4, :].bitcast(I32),
+                                tab2_scales[0, 4 * q:4 * q + 4, :].bitcast(I32))
+        g1 = keep.tile([P, PACK], F32, name="g1")
+        nc.gpsimd.dma_start(g1[:], gain1.rearrange("(p t) -> p t", t=PACK))
+        g2 = keep.tile([P, PACK], F32, name="g2")
+        nc.gpsimd.dma_start(g2[:], gain2.rearrange("(p t) -> p t", t=PACK))
+        for q in range(QUADS):
+            nc.gpsimd.dma_start(w3_sc[32 * q + W3_ROW:32 * q + W3_ROW + 4, :].bitcast(I32),
+                                w3_scales[0, 4 * q:4 * q + 4, :].bitcast(I32))
+
+        w1_w = keep.tile([P, PASSES, 2 * H], U8, name="w1_w", align_bytes=64)
+        nc.scalar.copy(w1_w[:].bitcast(U16).rearrange("p a (t m) -> p a t m", t=PACK),
+                       w1_raw[:].bitcast(U16).rearrange("p a (m t) -> p a t m", t=PACK))
+        w1_sc = keep.tile([P, PASSES, H], U8, name="w1_sc", align_bytes=64)
+        nc.vector.tensor_copy(w1_sc[:].rearrange("p a (t m) -> p a t m", t=PACK),
+                              w1_sc_raw[:].rearrange("p (a m t) -> p a t m", a=PASSES, t=PACK))
+
+        bias = keep.tile([P, M_TILES], F32, name="bias", tag="w1_sc_raw", align_bytes=64)
+        with nc.allow_non_contiguous_dma(reason="one margin a partition"):
+            nc.gpsimd.dma_start(bias[:], margin.rearrange("(j p) -> p j", p=P))
+
+        v_sc = keep.tile([P, S], U8, name="v_sc", align_bytes=64)
+        nc.vector.tensor_copy(v_sc[:], tab_sc[:].indirect(idx[:]))
+        for q in range(QUADS):
+            nc.scalar.dma_start(v_sc1[32 * q:32 * q + 4, :].bitcast(I32), v_sc[32 * q + 4:32 * q + 8, :].bitcast(I32))
+        v_planes = [v_sc, v_sc1]
+
+        v_w = [keep.tile([P, S], U32, name=f"v_w{a}", align_bytes=64) for a in range(PASSES)]
+
+        def gather_words(a):
+            for hf in range(HALVES):
+                nc.vector.tensor_copy(v_w[a][:, hf * BANK:(hf + 1) * BANK],
+                                      tab_w[a][:].indirect(idx[:, hf * BANK // 16:(hf + 1) * BANK // 16]))
+
+        def first_stage_pass(bank, strip, a, weight, plane):
+            cols = slice(strip * STRIP, (strip + 1) * STRIP)
+            for t in range(PACK):
+                nc.tensor.matmul_mx(out=bank[:, t, :], lhsT=weight(a, t), lhsT_scale=plane[:, a, t * P:(t + 1) * P],
+                                    rhs=v_w[a][:, cols].bitcast(FP8X4), rhs_scale=v_planes[a][:, cols],
+                                    start=(a == 0 and t == 0), stop=(a == PASSES - 1 and t == PACK - 1))
+
+        def w1_slice(a, t):
+            return w1_w[:, a, 2 * t * P:2 * (t + 1) * P].bitcast(FP4X4)
+
+        gather_words(0)
+        h_banks = [psum.tile([P, PACK, STRIP], F32, name="bank", tag="bank") for strip in range(STRIPS)]
+        for strip in range(STRIPS):
+            first_stage_pass(h_banks[strip], strip, 0, w1_slice, w1_sc)
+        v2_sc = keep.tile([P, S2], U8, name="v2_sc", align_bytes=64)
+        nc.vector.tensor_copy(v2_sc[:], tab2_sc[:].indirect(idx2[:]))
+        gather_words(1)
+
+        w2_raw = ring.tile([P, PASSES, PACK, H], F32, name="w2_raw", tag="big", align_bytes=64)
+        for a in range(PASSES):
+            nc.sync.dma_start(w2_raw[:, a], w2[a * BANK:(a + 1) * BANK, :].rearrange("(p j) c -> p j c", j=PACK))
+        tab2_w = ring.tile([P, T3], U32, name="tab2_w", tag="big", align_bytes=64)
+        nc.sync.dma_start(tab2_w[:].bitcast(I32), words_of(tab2_words[0]))
+
+        w2_w = keep.tile([P, PASSES, H], U32, name="w2_w", align_bytes=64)
+        w2_sc = keep.tile([P, PASSES, H], U8, name="w2_sc", align_bytes=64)
+        w2_bf = [ring.tile([P, H * PACK], BF16, name="w2_bf", tag="w2_bf", align_bytes=64) for a in range(PASSES)]
+        for a in range(PASSES):
+            nc.vector.tensor_copy(w2_bf[a][:].rearrange("p (t m j) -> p m t j", t=PACK, j=PACK),
+                                  w2_raw[:, a].rearrange("p j (m t) -> p m t j", t=PACK))
+        for a in range(PASSES):
+            nc.vector.quantize_mx(out=w2_w[:, a, :].bitcast(FP8X4), scales=w2_sc[:, a, :], in_=w2_bf[a][:])
+        fit_sb = ring.tile([P, M_TILES, NP], F32, name="fit_sb", tag="big", align_bytes=64)
+        w3_w = ring.tile([P, S2], U32, name="w3_w", tag="w2_bf", align_bytes=64)
+        nc.sync.dma_start(w3_w[:].bitcast(I32), words_of(w3_words[0]))
+        nc.sync.dma_start(fit_sb[:], fit.rearrange("(j p) n -> p j n", p=P))
+
+        def w2_slice(a, t):
+            return w2_w[:, a, t * P:(t + 1) * P].bitcast(FP8X4)
+
+        def spread(gain):
+            return gain[:].unsqueeze(1).to_broadcast([P, 2 * STRIP, PACK])
+
+        def as_words(tile, pair):
+            return tile[:, pair * 2 * BANK:(pair + 1) * 2 * BANK].rearrange("p (n t) -> p n t", t=PACK)
+
+        h_w = keep.tile([P, S], U32, name="h_w", align_bytes=64)
+        h_sc = keep.tile([P, S], U8, name="h_sc", align_bytes=64)
+        f_w = keep.tile([P, S], U32, name="f_w", align_bytes=64)
+        f_sc = keep.tile([P, S], U8, name="f_sc", align_bytes=64)
+
+        def quantise_half(rounded, words, plane, hf):
+            cols = slice(hf * BANK, (hf + 1) * BANK)
+            nc.vector.quantize_mx(out=words[:, cols].bitcast(FP8X4), scales=plane[:, cols], in_=rounded[:])
+
+        strips_a_half = STRIPS // HALVES
+        for hf in range(HALVES):
+            act = ring.tile([P, PACK * BANK], F32, name="act", tag="act")
+            for i in range(strips_a_half):
+                strip = hf * strips_a_half + i
+                first_stage_pass(h_banks[strip], strip, 1, w1_slice, w1_sc)
+                nc.scalar.activation(act[:, i * BANK:(i + 1) * BANK].rearrange("p (n t) -> p n t", t=PACK),
+                                     h_banks[strip][:].rearrange("p t n -> p n t"), ACT.Tanh)
+            rounded = ring.tile([P, PACK * BANK], BF16, name="rounded", tag="rounded", align_bytes=64)
+            for pair in range(2):
+                nc.vector.tensor_tensor(as_words(rounded, pair), as_words(act, pair), spread(g1), ALU.mult)
+            quantise_half(rounded, h_w, h_sc, hf)
+
+        g2_twice = keep.tile([P, PACK], F32, name="g2_twice")
+        nc.vector.tensor_scalar(g2_twice[:], g2[:], 2.0, None, ALU.mult)
+        for hf in range(HALVES):
+            act = ring.tile([P, PACK * BANK], F32, name="act", tag="act")
+            for i in range(strips_a_half):
+                strip = hf * strips_a_half + i
+                bank = psum.tile([P, PACK, STRIP], F32, name="bank", tag="bank")
+                for a in range(PASSES):
+                    first_stage_pass(bank, strip, a, w2_slice, w2_sc)
+                sine = ring.tile([P, BANK], F32, name="sine", tag="scalar_out")
+                nc.scalar.activation(sine[:].rearrange("p (n t) -> p n t", t=PACK), bank[:].rearrange("p t n -> p n t"),
+                                     ACT.Sin, bias=quarter_pi[:], scale=0.5)
+                nc.scalar.activation(act[:, i * BANK:(i + 1) * BANK], sine[:], ACT.Square)
+            rounded = ring.tile([P, PACK * BANK], BF16, name="rounded", tag="rounded", align_bytes=64)
+            for pair in range(2):
+                nc.vector.scalar_tensor_tensor(as_words(rounded, pair), as_words(act, pair), 0.5, spread(g2_twice),
+                                               ALU.subtract, ALU.mult)
+            quantise_half(rounded, f_w, f_sc, hf)
+
+        v2_w = keep.tile([P, S2], U32, name="v2_w", align_bytes=64)
+        nc.vector.tensor_copy(v2_w[:], tab2_w[:].indirect(idx2[:]))
+
+        def scores(j, stationary, plane, row, words, moving_plane, name, on_vector):
+            rows = slice(j * P, (j + 1) * P)
+            whole = keep.tile([P, S], F32, name=f"{name}{j}")
+            for hf in range(HALVES):
+                cols = slice(hf * BANK, (hf + 1) * BANK)
+                bank = psum.tile([P, BANK], F32, name="bank", tag="bank")
+                nc.tensor.matmul_mx(out=bank[:], lhsT=stationary[:, rows].bitcast(FP8X4), lhsT_scale=plane[row:P, rows],
+                                    rhs=words[:, cols].bitcast(FP8X4), rhs_scale=moving_plane[:, cols],
+                                    start=True, stop=True)
+                if on_vector:
+                    nc.vector.tensor_copy(whole[:, cols], bank[:])
+                else:
+                    nc.scalar.copy(whole[:, cols], bank[:])
+            return whole
+
+        e_tiles = [scores(j, v2_w, v2_sc, V2_ROW, h_w, h_sc, "e", True) for j in range(E_ON_VECTOR)]
+        for j in range(M_TILES):
+            d_tile = scores(j, w3_w, w3_sc, W3_ROW, f_w, f_sc, "d", False)
+            if j + E_ON_VECTOR < M_TILES:
+                e_tiles.append(scores(j + E_ON_VECTOR, v2_w, v2_sc, V2_ROW, h_w, h_sc, "e", False))
+            gate = ring.tile([P, NP], F32, name="gate", tag="scalar_out")
+            nc.scalar.activation(gate[:], e_tiles[j][:].indirect(p1[:]), ACT.Sigmoid, bias=bias[:, j:j + 1])
+            picked = ring.tile([P, NP], F32, name="picked", tag="picked")
+            nc.vector.tensor_copy(picked[:], d_tile[:].indirect(p2[:]))
+            gated = ring.tile([P, NP], F32, name="gated", tag="gated")
+            nc.vector.tensor_tensor(gated[:], gate[:], fit_sb[:, j, :], ALU.mult)
+            best = keep.tile([P, NP], F32, name=f"best{j}")
+            nc.vector.tensor_tensor(best[:], gated[:], picked[:], ALU.max)
+            nc.sync.dma_start(out[j * P:(j + 1) * P, :], best[:])

@@ -28,7 +28,11 @@ HALVES = S // BANK
 M_TILES = S2 // P
 V2_ROW = 8
 W3_ROW = 12
-E_ON_VECTOR = 5
+SPARE_ROW = 4
+SPARE_STEP = 8
+LAG = 1
+E_V = [()] * 8
+D_V = [(0, 1)] * 3 + [()] * 5
 
 
 def tile_list_berth_filling_kernel(tc, tab_words, tab_scales, offs, tab2_words, tab2_scales, offs2,
@@ -38,8 +42,15 @@ def tile_list_berth_filling_kernel(tc, tab_words, tab_scales, offs, tab2_words, 
     with ExitStack() as ctx:
         lists = ctx.enter_context(tc.tile_pool(name="lists", bufs=1))
         keep = ctx.enter_context(tc.tile_pool(name="keep", bufs=1))
+        shared = ctx.enter_context(tc.tile_pool(name="shared", bufs=1))
         ring = ctx.enter_context(tc.tile_pool(name="ring", bufs=2))
-        psum = ctx.enter_context(tc.psum_pool(name="psum", bufs=8))
+        psum = ctx.enter_context(tc.psum_pool(name="psum", bufs=1))
+
+        used = []
+
+        def next_bank(shape):
+            used.append(psum.tile(shape, F32, name="bank", tag=f"bank{len(used) % 8}"))
+            return used[-1]
 
         def words_of(dram):
             return dram.rearrange("p n t -> p (n t)").bitcast(I32)
@@ -54,66 +65,60 @@ def tile_list_berth_filling_kernel(tc, tab_words, tab_scales, offs, tab2_words, 
             engine.memset(tile[:].bitcast(I32), 0)
             return tile
 
-        tab_sc = zeroed_plane([P, T], "tab_sc", nc.vector)
-        ones = ring.tile([P, 1], F32, name="ones", tag="big", align_bytes=64)
-        nc.vector.memset(ones[:], 1.0)
-        quarter_pi = keep.tile([P, 1], F32, name="quarter_pi")
-        nc.vector.tensor_scalar(quarter_pi[:], ones[:], math.pi / 4, None, ALU.mult)
-        w1_sc_raw = zeroed_plane([P, PASSES * H], "w1_sc_raw", nc.gpsimd, tag="w1_sc_raw")
-        for q in range(QUADS):
-            nc.gpsimd.dma_start(w1_sc_raw[32 * q:32 * q + 4, :].bitcast(I32).rearrange("r (a n) -> r a n", a=PASSES),
-                                w1_scales[:, 4 * q:4 * q + 4, :].bitcast(I32).rearrange("a r n -> r a n"))
-        v_sc1 = zeroed_plane([P, S], "v_sc1", nc.vector)
-        tab2_sc = zeroed_plane([P, T3], "tab2_sc", nc.vector)
-        w3_sc = zeroed_plane([P, S2], "w3_sc", nc.vector)
-        tab_w = [ring.tile([P, T], U32, name="tab_w", tag="big", align_bytes=64) for a in range(PASSES)]
-
+        tab_w = [None] * PASSES
         idx = load_list(offs, "idx")
-        w1_raw = keep.tile([P, PASSES, 2 * H], U8, name="w1_raw")
-        nc.sync.dma_start(w1_raw[:].bitcast(I32), w1_words.rearrange("a p n -> p a n").bitcast(I32))
         idx2 = load_list(offs2, "idx2")
-        nc.sync.dma_start(tab_w[0][:].bitcast(I32), words_of(tab_words[0]))
         p1 = load_list(pos1, "p1")
         p2 = load_list(pos2, "p2")
-        for q in range(QUADS):
-            nc.scalar.dma_start(tab_sc[32 * q:32 * q + 4 * PASSES, :].bitcast(I32),
-                                tab_scales[:, 4 * q:4 * q + 4, :].bitcast(I32))
-        nc.sync.dma_start(tab_w[1][:].bitcast(I32), words_of(tab_words[1]))
+        w1_raw = keep.tile([P, PASSES, 2 * H], U8, name="w1_raw", tag="big1", align_bytes=64)
+        nc.sync.dma_start(w1_raw[:].bitcast(I32), w1_words.rearrange("a p n -> p a n").bitcast(I32))
+        tab_w[0] = keep.tile([P, T], U32, name="tab_w0", tag="big0", align_bytes=64)
+        nc.sync.dma_start(tab_w[0][:].bitcast(I32), words_of(tab_words[0]))
 
-        for q in range(QUADS):
-            nc.gpsimd.dma_start(tab2_sc[32 * q + V2_ROW:32 * q + V2_ROW + 4, :].bitcast(I32),
-                                tab2_scales[0, 4 * q:4 * q + 4, :].bitcast(I32))
-        g1 = keep.tile([P, PACK], F32, name="g1")
-        nc.gpsimd.dma_start(g1[:], gain1.rearrange("(p t) -> p t", t=PACK))
-        g2 = keep.tile([P, PACK], F32, name="g2")
-        nc.gpsimd.dma_start(g2[:], gain2.rearrange("(p t) -> p t", t=PACK))
-        for q in range(QUADS):
-            nc.gpsimd.dma_start(w3_sc[32 * q + W3_ROW:32 * q + W3_ROW + 4, :].bitcast(I32),
-                                w3_scales[0, 4 * q:4 * q + 4, :].bitcast(I32))
+        w1_sc_raw = shared.tile([P, PASSES * H], U8, name="w1_sc_raw", offset=4 * S - H, align_bytes=64)
+        nc.gpsimd.memset(w1_sc_raw[:].bitcast(I32), 0)
+        tab_sc = zeroed_plane([P, T], "tab_sc", nc.vector, tag="planes")
+        ones = keep.tile([P, 1], F32, name="ones", tag="gains", align_bytes=64)
+        nc.vector.memset(ones[:], 1.0)
+        tab2_sc = zeroed_plane([P, T3], "tab2_sc", nc.vector)
 
-        w1_w = keep.tile([P, PASSES, 2 * H], U8, name="w1_w", align_bytes=64)
+        nc.scalar.dma_start(tab_sc[SPARE_ROW:P:SPARE_STEP, :].bitcast(I32), tab_scales[1].bitcast(I32))
+        for q in range(QUADS):
+            nc.scalar.dma_start(tab_sc[32 * q:32 * q + 4, :].bitcast(I32), tab_scales[0, 4 * q:4 * q + 4, :].bitcast(I32))
+        quarter_pi = keep.tile([P, 1], F32, name="quarter_pi", tag="column", align_bytes=64)
+        nc.scalar.activation(quarter_pi[:], ones[:], ACT.Identity, scale=math.pi / 4)
+        for q in range(QUADS):
+            (nc.gpsimd if q else nc.scalar).dma_start(w1_sc_raw[32 * q:32 * q + 4, :].bitcast(I32).rearrange("r (a n) -> r a n", a=PASSES),
+                                w1_scales[:, 4 * q:4 * q + 4, :].bitcast(I32).rearrange("a r n -> r a n"))
+        gains = keep.tile([P, 2, 2 * PACK], F32, name="gains", tag="gains", align_bytes=64)
+        g1, g2 = gains[:, 0, 0:PACK], gains[:, 1, 0:PACK]
+        nc.gpsimd.dma_start(g1, gain1.rearrange("(p t) -> p t", t=PACK))
+        nc.gpsimd.dma_start(g2, gain2.rearrange("(p t) -> p t", t=PACK))
+
+        w1_w = keep.tile([P, PASSES, 2 * H], U8, name="w1_w", tag="w1_w", align_bytes=64)
         nc.scalar.copy(w1_w[:].bitcast(U16).rearrange("p a (t m) -> p a t m", t=PACK),
                        w1_raw[:].bitcast(U16).rearrange("p a (m t) -> p a t m", t=PACK))
-        w1_sc = keep.tile([P, PASSES, H], U8, name="w1_sc", align_bytes=64)
+        tab_w[1] = keep.tile([P, T], U32, name="tab_w1", tag="big1", align_bytes=64)
+        nc.sync.dma_start(tab_w[1][:].bitcast(I32), words_of(tab_words[1]))
+
+        v_sc = keep.tile([P, S], U8, name="v_sc", align_bytes=64)
+        v_sc1 = keep.tile([P, S], U8, name="v_sc1", align_bytes=64)
+        nc.vector.tensor_copy(v_sc[:], tab_sc[:].indirect(idx[:]))
+        for q in range(QUADS):
+            nc.scalar.dma_start(v_sc1[32 * q:32 * q + 4, :].bitcast(I32),
+                                v_sc[32 * q + SPARE_ROW:32 * q + 32:SPARE_STEP, :].bitcast(I32))
+        v_planes = [v_sc, v_sc1]
+
+        w1_sc = keep.tile([P, PASSES, H], U8, name="w1_sc", tag="planes", align_bytes=64)
         nc.vector.tensor_copy(w1_sc[:].rearrange("p a (t m) -> p a t m", t=PACK),
                               w1_sc_raw[:].rearrange("p (a m t) -> p a t m", a=PASSES, t=PACK))
 
-        bias = keep.tile([P, M_TILES], F32, name="bias", tag="w1_sc_raw", align_bytes=64)
-        with nc.allow_non_contiguous_dma(reason="one margin a partition"):
-            nc.gpsimd.dma_start(bias[:], margin.rearrange("(j p) -> p j", p=P))
+        v_w = [shared.tile([P, S], U32, name="v_w0", offset=0, align_bytes=64),
+               keep.tile([P, S], U32, name="v_w1", tag="big0", align_bytes=64)]
 
-        v_sc = keep.tile([P, S], U8, name="v_sc", align_bytes=64)
-        nc.vector.tensor_copy(v_sc[:], tab_sc[:].indirect(idx[:]))
-        for q in range(QUADS):
-            nc.scalar.dma_start(v_sc1[32 * q:32 * q + 4, :].bitcast(I32), v_sc[32 * q + 4:32 * q + 8, :].bitcast(I32))
-        v_planes = [v_sc, v_sc1]
-
-        v_w = [keep.tile([P, S], U32, name=f"v_w{a}", align_bytes=64) for a in range(PASSES)]
-
-        def gather_words(a):
-            for hf in range(HALVES):
-                nc.vector.tensor_copy(v_w[a][:, hf * BANK:(hf + 1) * BANK],
-                                      tab_w[a][:].indirect(idx[:, hf * BANK // 16:(hf + 1) * BANK // 16]))
+        def gather_words(a, cuts):
+            for lo, hi in zip(cuts, cuts[1:]):
+                nc.vector.tensor_copy(v_w[a][:, lo:hi], tab_w[a][:].indirect(idx[:, lo // 16:hi // 16]))
 
         def first_stage_pass(bank, strip, a, weight, plane):
             cols = slice(strip * STRIP, (strip + 1) * STRIP)
@@ -125,38 +130,36 @@ def tile_list_berth_filling_kernel(tc, tab_words, tab_scales, offs, tab2_words, 
         def w1_slice(a, t):
             return w1_w[:, a, 2 * t * P:2 * (t + 1) * P].bitcast(FP4X4)
 
-        gather_words(0)
-        h_banks = [psum.tile([P, PACK, STRIP], F32, name="bank", tag="bank") for strip in range(STRIPS)]
+        gather_words(0, (0, BANK, S))
+        h_banks = [next_bank([P, PACK, STRIP]) for strip in range(STRIPS)]
         for strip in range(STRIPS):
             first_stage_pass(h_banks[strip], strip, 0, w1_slice, w1_sc)
-        v2_sc = keep.tile([P, S2], U8, name="v2_sc", align_bytes=64)
-        nc.vector.tensor_copy(v2_sc[:], tab2_sc[:].indirect(idx2[:]))
-        gather_words(1)
+        gather_words(1, (0, 2 * STRIP, BANK, S))
 
-        w2_raw = ring.tile([P, PASSES, PACK, H], F32, name="w2_raw", tag="big", align_bytes=64)
+        w2_raw = shared.tile([P, PASSES, PACK, H], F32, name="w2_raw", offset=4 * S, align_bytes=64)
         for a in range(PASSES):
             nc.sync.dma_start(w2_raw[:, a], w2[a * BANK:(a + 1) * BANK, :].rearrange("(p j) c -> p j c", j=PACK))
-        tab2_w = ring.tile([P, T3], U32, name="tab2_w", tag="big", align_bytes=64)
-        nc.sync.dma_start(tab2_w[:].bitcast(I32), words_of(tab2_words[0]))
 
         w2_w = keep.tile([P, PASSES, H], U32, name="w2_w", align_bytes=64)
         w2_sc = keep.tile([P, PASSES, H], U8, name="w2_sc", align_bytes=64)
-        w2_bf = [ring.tile([P, H * PACK], BF16, name="w2_bf", tag="w2_bf", align_bytes=64) for a in range(PASSES)]
-        for a in range(PASSES):
-            nc.vector.tensor_copy(w2_bf[a][:].rearrange("p (t m j) -> p m t j", t=PACK, j=PACK),
-                                  w2_raw[:, a].rearrange("p j (m t) -> p m t j", t=PACK))
-        for a in range(PASSES):
-            nc.vector.quantize_mx(out=w2_w[:, a, :].bitcast(FP8X4), scales=w2_sc[:, a, :], in_=w2_bf[a][:])
-        fit_sb = ring.tile([P, M_TILES, NP], F32, name="fit_sb", tag="big", align_bytes=64)
-        w3_w = ring.tile([P, S2], U32, name="w3_w", tag="w2_bf", align_bytes=64)
-        nc.sync.dma_start(w3_w[:].bitcast(I32), words_of(w3_words[0]))
-        nc.sync.dma_start(fit_sb[:], fit.rearrange("(j p) n -> p j n", p=P))
+        pieces = [(0, 0, PACK), (1, 0, PACK // 2), (1, PACK // 2, PACK)]
+        w2_bf = [keep.tile([P, (hi - lo) * BANK], BF16, name="w2_bf", tag=f"w2_bf{i}", align_bytes=64)
+                 for i, (a, lo, hi) in enumerate(pieces)]
+        for i, (a, lo, hi) in enumerate(pieces):
+            nc.vector.tensor_copy(w2_bf[i][:].rearrange("p (t m j) -> p m t j", m=P, j=PACK),
+                                  w2_raw[:, a].rearrange("p j (m t) -> p m t j", t=PACK)[:, :, lo:hi, :])
+        for i, (a, lo, hi) in enumerate(pieces):
+            nc.vector.quantize_mx(out=w2_w[:, a, lo * P:hi * P].bitcast(FP8X4), scales=w2_sc[:, a, lo * P:hi * P],
+                                  in_=w2_bf[i][:])
+
+        tab2_w = keep.tile([P, T3], U32, name="tab2_w", tag="big1", align_bytes=64)
+        nc.sync.dma_start(tab2_w[:].bitcast(I32), words_of(tab2_words[0]))
 
         def w2_slice(a, t):
             return w2_w[:, a, t * P:(t + 1) * P].bitcast(FP8X4)
 
         def spread(gain):
-            return gain[:].unsqueeze(1).to_broadcast([P, 2 * STRIP, PACK])
+            return gain.unsqueeze(1).to_broadcast([P, 2 * STRIP, PACK])
 
         def as_words(tile, pair):
             return tile[:, pair * 2 * BANK:(pair + 1) * 2 * BANK].rearrange("p (n t) -> p n t", t=PACK)
@@ -168,69 +171,94 @@ def tile_list_berth_filling_kernel(tc, tab_words, tab_scales, offs, tab2_words, 
 
         def quantise_half(rounded, words, plane, hf):
             cols = slice(hf * BANK, (hf + 1) * BANK)
-            nc.vector.quantize_mx(out=words[:, cols].bitcast(FP8X4), scales=plane[:, cols], in_=rounded[:])
+            nc.vector.quantize_mx(out=words[:, cols].bitcast(FP8X4), scales=plane[:, cols], in_=rounded[:, :])
 
         strips_a_half = STRIPS // HALVES
+        h_rounded = keep.tile([P, HALVES * PACK * BANK], BF16, name="h_rounded", tag="w2_bf2", align_bytes=64)
         for hf in range(HALVES):
-            act = ring.tile([P, PACK * BANK], F32, name="act", tag="act")
+            act = ring.tile([P, PACK * BANK], F32, name="act", tag="act", bufs=4)
             for i in range(strips_a_half):
                 strip = hf * strips_a_half + i
-                first_stage_pass(h_banks[strip], strip, 1, w1_slice, w1_sc)
+                bank = h_banks[strip]
+                first_stage_pass(bank, strip, 1, w1_slice, w1_sc)
                 nc.scalar.activation(act[:, i * BANK:(i + 1) * BANK].rearrange("p (n t) -> p n t", t=PACK),
-                                     h_banks[strip][:].rearrange("p t n -> p n t"), ACT.Tanh)
-            rounded = ring.tile([P, PACK * BANK], BF16, name="rounded", tag="rounded", align_bytes=64)
+                                     bank[:].rearrange("p t n -> p n t"), ACT.Tanh)
+            rounded = h_rounded[:, hf * PACK * BANK:(hf + 1) * PACK * BANK]
             for pair in range(2):
                 nc.vector.tensor_tensor(as_words(rounded, pair), as_words(act, pair), spread(g1), ALU.mult)
             quantise_half(rounded, h_w, h_sc, hf)
 
-        g2_twice = keep.tile([P, PACK], F32, name="g2_twice")
-        nc.vector.tensor_scalar(g2_twice[:], g2[:], 2.0, None, ALU.mult)
+        for q in range(QUADS):
+            nc.gpsimd.dma_start(tab2_sc[32 * q + V2_ROW:32 * q + V2_ROW + 4, :].bitcast(I32),
+                                tab2_scales[0, 4 * q:4 * q + 4, :].bitcast(I32))
+        v2_w = keep.tile([P, S2], U32, name="v2_w", align_bytes=64)
+        nc.vector.tensor_copy(v2_w[:], tab2_w[:].indirect(idx2[:]))
+        v2_sc = keep.tile([P, S2], U8, name="v2_sc", tag="w2_bf1", align_bytes=64)
+        nc.vector.tensor_copy(v2_sc[:], tab2_sc[:].indirect(idx2[:]))
+        w3_w = keep.tile([P, S2], U32, name="w3_w", tag="w2_bf0", align_bytes=64)
+        nc.sync.dma_start(w3_w[:].bitcast(I32), words_of(w3_words[0]))
+        w3_sc = keep.tile([P, S2], U8, name="w3_sc", tag="planes", align_bytes=64)
+        for q in range(QUADS):
+            nc.sync.dma_start(w3_sc[32 * q + W3_ROW:32 * q + W3_ROW + 4, :].bitcast(I32),
+                              w3_scales[0, 4 * q:4 * q + 4, :].bitcast(I32))
+        fit_sb = shared.tile([P, M_TILES, NP], F32, name="fit_sb", offset=4 * S, align_bytes=64)
+        nc.sync.dma_start(fit_sb[:], fit.rearrange("(j p) n -> p j n", p=P))
+
         for hf in range(HALVES):
-            act = ring.tile([P, PACK * BANK], F32, name="act", tag="act")
+            act = ring.tile([P, PACK * BANK], F32, name="act", tag="act", bufs=4)
             for i in range(strips_a_half):
                 strip = hf * strips_a_half + i
-                bank = psum.tile([P, PACK, STRIP], F32, name="bank", tag="bank")
+                bank = next_bank([P, PACK, STRIP])
                 for a in range(PASSES):
                     first_stage_pass(bank, strip, a, w2_slice, w2_sc)
-                sine = ring.tile([P, BANK], F32, name="sine", tag="scalar_out")
+                sine = ring.tile([P, BANK], F32, name="sine", tag="sine")
                 nc.scalar.activation(sine[:].rearrange("p (n t) -> p n t", t=PACK), bank[:].rearrange("p t n -> p n t"),
                                      ACT.Sin, bias=quarter_pi[:], scale=0.5)
-                nc.scalar.activation(act[:, i * BANK:(i + 1) * BANK], sine[:], ACT.Square)
+                nc.scalar.activation(act[:, i * BANK:(i + 1) * BANK], sine[:], ACT.Square, scale=math.sqrt(2.0))
             rounded = ring.tile([P, PACK * BANK], BF16, name="rounded", tag="rounded", align_bytes=64)
             for pair in range(2):
-                nc.vector.scalar_tensor_tensor(as_words(rounded, pair), as_words(act, pair), 0.5, spread(g2_twice),
+                nc.vector.scalar_tensor_tensor(as_words(rounded, pair), as_words(act, pair), 1.0, spread(g2),
                                                ALU.subtract, ALU.mult)
             quantise_half(rounded, f_w, f_sc, hf)
 
-        v2_w = keep.tile([P, S2], U32, name="v2_w", align_bytes=64)
-        nc.vector.tensor_copy(v2_w[:], tab2_w[:].indirect(idx2[:]))
+        bias = keep.tile([P, M_TILES], F32, name="bias", tag="column", align_bytes=64)
+        with nc.allow_non_contiguous_dma(reason="one margin a partition"):
+            nc.sync.dma_start(bias[:], margin.rearrange("(j p) -> p j", p=P))
 
         def scores(j, stationary, plane, row, words, moving_plane, name, on_vector):
             rows = slice(j * P, (j + 1) * P)
-            whole = keep.tile([P, S], F32, name=f"{name}{j}")
+            whole = ring.tile([P, S], F32, name=name, tag=name, bufs=4)
             for hf in range(HALVES):
                 cols = slice(hf * BANK, (hf + 1) * BANK)
-                bank = psum.tile([P, BANK], F32, name="bank", tag="bank")
+                bank = next_bank([P, BANK])
                 nc.tensor.matmul_mx(out=bank[:], lhsT=stationary[:, rows].bitcast(FP8X4), lhsT_scale=plane[row:P, rows],
                                     rhs=words[:, cols].bitcast(FP8X4), rhs_scale=moving_plane[:, cols],
                                     start=True, stop=True)
-                if on_vector:
+                if hf in on_vector:
                     nc.vector.tensor_copy(whole[:, cols], bank[:])
                 else:
                     nc.scalar.copy(whole[:, cols], bank[:])
             return whole
 
-        e_tiles = [scores(j, v2_w, v2_sc, V2_ROW, h_w, h_sc, "e", True) for j in range(E_ON_VECTOR)]
+        def look(j):
+            e_tile = scores(j, v2_w, v2_sc, V2_ROW, h_w, h_sc, "e", E_V[j])
+            gate = keep.tile([P, NP], F32, name=f"gate{j}")
+            nc.scalar.activation(gate[:], e_tile[:].indirect(p1[:]), ACT.Sigmoid, bias=bias[:, j:j + 1])
+            return gate
+
+        gates = [look(j) for j in range(LAG)]
         for j in range(M_TILES):
-            d_tile = scores(j, w3_w, w3_sc, W3_ROW, f_w, f_sc, "d", False)
-            if j + E_ON_VECTOR < M_TILES:
-                e_tiles.append(scores(j + E_ON_VECTOR, v2_w, v2_sc, V2_ROW, h_w, h_sc, "e", False))
-            gate = ring.tile([P, NP], F32, name="gate", tag="scalar_out")
-            nc.scalar.activation(gate[:], e_tiles[j][:].indirect(p1[:]), ACT.Sigmoid, bias=bias[:, j:j + 1])
-            picked = ring.tile([P, NP], F32, name="picked", tag="picked")
-            nc.vector.tensor_copy(picked[:], d_tile[:].indirect(p2[:]))
+            d_tile = scores(j, w3_w, w3_sc, W3_ROW, f_w, f_sc, "d", D_V[j])
+            if j + LAG < M_TILES:
+                gates.append(look(j + LAG))
+            gate = gates[j]
             gated = ring.tile([P, NP], F32, name="gated", tag="gated")
-            nc.vector.tensor_tensor(gated[:], gate[:], fit_sb[:, j, :], ALU.mult)
+            picked = ring.tile([P, NP], F32, name="picked", tag="picked")
             best = keep.tile([P, NP], F32, name=f"best{j}")
-            nc.vector.tensor_tensor(best[:], gated[:], picked[:], ALU.max)
-            nc.sync.dma_start(out[j * P:(j + 1) * P, :], best[:])
+            nc.vector.tensor_tensor(gated[:], gate[:], fit_sb[:, j, :], ALU.mult)
+            nc.vector.tensor_copy(picked[:], d_tile[:].indirect(p2[:]))
+            pieces = 2 if j == M_TILES - 1 else 1
+            for i in range(pieces):
+                cols = slice(i * NP // pieces, (i + 1) * NP // pieces)
+                nc.vector.tensor_tensor(best[:, cols], gated[:, cols], picked[:, cols], ALU.max)
+                nc.sync.dma_start(out[j * P:(j + 1) * P, cols], best[:, cols])

import math
from contextlib import ExitStack

import concourse.mybir as mybir

K, H, T, S, T3, S2, NP = 1024, 512, 4096, 1024, 2048, 1024, 512
FLOPS = 2 * (2 * K * H * S + 2 * H * S2 * S)

F32 = mybir.dt.float32
BF16 = mybir.dt.bfloat16
I32 = mybir.dt.int32
U32 = mybir.dt.uint32
U16 = mybir.dt.uint16
U8 = mybir.dt.uint8
FP8X4 = mybir.dt.float8_e4m3fn_x4
FP4X4 = mybir.dt.float4_e2m1fn_x4
ACT = mybir.ActivationFunctionType
ALU = mybir.AluOpType

P = 128
PACK = 4
QUADS = 4
PASSES = K // (P * PACK)
BANK = 512
STRIP = BANK // PACK
STRIPS = S // STRIP
HALVES = S // BANK
M_TILES = S2 // P
V2_ROW = 8
W3_ROW = 12
SPARE_ROW = 4
SPARE_STEP = 8
LAG = 1
E_V = [()] * 8
D_V = [(0, 1)] * 3 + [()] * 5


def tile_list_berth_filling_kernel(tc, tab_words, tab_scales, offs, tab2_words, tab2_scales, offs2,
                                             pos1, pos2, w1_words, w1_scales, w2, w3_words, w3_scales,
                                             gain1, gain2, margin, fit, out):
    nc = tc.nc
    with ExitStack() as ctx:
        lists = ctx.enter_context(tc.tile_pool(name="lists", bufs=1))
        keep = ctx.enter_context(tc.tile_pool(name="keep", bufs=1))
        shared = ctx.enter_context(tc.tile_pool(name="shared", bufs=1))
        ring = ctx.enter_context(tc.tile_pool(name="ring", bufs=2))
        psum = ctx.enter_context(tc.psum_pool(name="psum", bufs=1))

        used = []

        def next_bank(shape):
            used.append(psum.tile(shape, F32, name="bank", tag=f"bank{len(used) % 8}"))
            return used[-1]

        def words_of(dram):
            return dram.rearrange("p n t -> p (n t)").bitcast(I32)

        def load_list(dram, name):
            tile = lists.tile(list(dram.shape), U16, name=name)
            nc.sync.dma_start(tile[:], dram)
            return tile

        def zeroed_plane(shape, name, engine, tag=None):
            tile = keep.tile(shape, U8, name=name, tag=tag or name, align_bytes=64)
            engine.memset(tile[:].bitcast(I32), 0)
            return tile

        tab_w = [None] * PASSES
        idx = load_list(offs, "idx")
        idx2 = load_list(offs2, "idx2")
        p1 = load_list(pos1, "p1")
        p2 = load_list(pos2, "p2")
        w1_raw = keep.tile([P, PASSES, 2 * H], U8, name="w1_raw", tag="big1", align_bytes=64)
        nc.sync.dma_start(w1_raw[:].bitcast(I32), w1_words.rearrange("a p n -> p a n").bitcast(I32))
        tab_w[0] = keep.tile([P, T], U32, name="tab_w0", tag="big0", align_bytes=64)
        nc.sync.dma_start(tab_w[0][:].bitcast(I32), words_of(tab_words[0]))

        w1_sc_raw = shared.tile([P, PASSES * H], U8, name="w1_sc_raw", offset=4 * S - H, align_bytes=64)
        nc.gpsimd.memset(w1_sc_raw[:].bitcast(I32), 0)
        tab_sc = zeroed_plane([P, T], "tab_sc", nc.vector, tag="planes")
        ones = keep.tile([P, 1], F32, name="ones", tag="gains", align_bytes=64)
        nc.vector.memset(ones[:], 1.0)
        tab2_sc = zeroed_plane([P, T3], "tab2_sc", nc.vector)

        nc.scalar.dma_start(tab_sc[SPARE_ROW:P:SPARE_STEP, :].bitcast(I32), tab_scales[1].bitcast(I32))
        for q in range(QUADS):
            nc.scalar.dma_start(tab_sc[32 * q:32 * q + 4, :].bitcast(I32), tab_scales[0, 4 * q:4 * q + 4, :].bitcast(I32))
        quarter_pi = keep.tile([P, 1], F32, name="quarter_pi", tag="column", align_bytes=64)
        nc.scalar.activation(quarter_pi[:], ones[:], ACT.Identity, scale=math.pi / 4)
        for q in range(QUADS):
            (nc.gpsimd if q else nc.scalar).dma_start(w1_sc_raw[32 * q:32 * q + 4, :].bitcast(I32).rearrange("r (a n) -> r a n", a=PASSES),
                                w1_scales[:, 4 * q:4 * q + 4, :].bitcast(I32).rearrange("a r n -> r a n"))
        gains = keep.tile([P, 2, 2 * PACK], F32, name="gains", tag="gains", align_bytes=64)
        g1, g2 = gains[:, 0, 0:PACK], gains[:, 1, 0:PACK]
        nc.gpsimd.dma_start(g1, gain1.rearrange("(p t) -> p t", t=PACK))
        nc.gpsimd.dma_start(g2, gain2.rearrange("(p t) -> p t", t=PACK))

        w1_w = keep.tile([P, PASSES, 2 * H], U8, name="w1_w", tag="w1_w", align_bytes=64)
        nc.scalar.copy(w1_w[:].bitcast(U16).rearrange("p a (t m) -> p a t m", t=PACK),
                       w1_raw[:].bitcast(U16).rearrange("p a (m t) -> p a t m", t=PACK))
        tab_w[1] = keep.tile([P, T], U32, name="tab_w1", tag="big1", align_bytes=64)
        nc.sync.dma_start(tab_w[1][:].bitcast(I32), words_of(tab_words[1]))

        v_sc = keep.tile([P, S], U8, name="v_sc", align_bytes=64)
        v_sc1 = keep.tile([P, S], U8, name="v_sc1", align_bytes=64)
        nc.vector.tensor_copy(v_sc[:], tab_sc[:].indirect(idx[:]))
        for q in range(QUADS):
            nc.scalar.dma_start(v_sc1[32 * q:32 * q + 4, :].bitcast(I32),
                                v_sc[32 * q + SPARE_ROW:32 * q + 32:SPARE_STEP, :].bitcast(I32))
        v_planes = [v_sc, v_sc1]

        w1_sc = keep.tile([P, PASSES, H], U8, name="w1_sc", tag="planes", align_bytes=64)
        nc.vector.tensor_copy(w1_sc[:].rearrange("p a (t m) -> p a t m", t=PACK),
                              w1_sc_raw[:].rearrange("p (a m t) -> p a t m", a=PASSES, t=PACK))

        v_w = [shared.tile([P, S], U32, name="v_w0", offset=0, align_bytes=64),
               keep.tile([P, S], U32, name="v_w1", tag="big0", align_bytes=64)]

        def gather_words(a, cuts):
            for lo, hi in zip(cuts, cuts[1:]):
                nc.vector.tensor_copy(v_w[a][:, lo:hi], tab_w[a][:].indirect(idx[:, lo // 16:hi // 16]))

        def first_stage_pass(bank, strip, a, weight, plane):
            cols = slice(strip * STRIP, (strip + 1) * STRIP)
            for t in range(PACK):
                nc.tensor.matmul_mx(out=bank[:, t, :], lhsT=weight(a, t), lhsT_scale=plane[:, a, t * P:(t + 1) * P],
                                    rhs=v_w[a][:, cols].bitcast(FP8X4), rhs_scale=v_planes[a][:, cols],
                                    start=(a == 0 and t == 0), stop=(a == PASSES - 1 and t == PACK - 1))

        def w1_slice(a, t):
            return w1_w[:, a, 2 * t * P:2 * (t + 1) * P].bitcast(FP4X4)

        gather_words(0, (0, BANK, S))
        h_banks = [next_bank([P, PACK, STRIP]) for strip in range(STRIPS)]
        for strip in range(STRIPS):
            first_stage_pass(h_banks[strip], strip, 0, w1_slice, w1_sc)
        gather_words(1, (0, 2 * STRIP, BANK, S))

        w2_raw = shared.tile([P, PASSES, PACK, H], F32, name="w2_raw", offset=4 * S, align_bytes=64)
        for a in range(PASSES):
            nc.sync.dma_start(w2_raw[:, a], w2[a * BANK:(a + 1) * BANK, :].rearrange("(p j) c -> p j c", j=PACK))

        w2_w = keep.tile([P, PASSES, H], U32, name="w2_w", align_bytes=64)
        w2_sc = keep.tile([P, PASSES, H], U8, name="w2_sc", align_bytes=64)
        pieces = [(0, 0, PACK), (1, 0, PACK // 2), (1, PACK // 2, PACK)]
        w2_bf = [keep.tile([P, (hi - lo) * BANK], BF16, name="w2_bf", tag=f"w2_bf{i}", align_bytes=64)
                 for i, (a, lo, hi) in enumerate(pieces)]
        for i, (a, lo, hi) in enumerate(pieces):
            nc.vector.tensor_copy(w2_bf[i][:].rearrange("p (t m j) -> p m t j", m=P, j=PACK),
                                  w2_raw[:, a].rearrange("p j (m t) -> p m t j", t=PACK)[:, :, lo:hi, :])
        for i, (a, lo, hi) in enumerate(pieces):
            nc.vector.quantize_mx(out=w2_w[:, a, lo * P:hi * P].bitcast(FP8X4), scales=w2_sc[:, a, lo * P:hi * P],
                                  in_=w2_bf[i][:])

        tab2_w = keep.tile([P, T3], U32, name="tab2_w", tag="big1", align_bytes=64)
        nc.sync.dma_start(tab2_w[:].bitcast(I32), words_of(tab2_words[0]))

        def w2_slice(a, t):
            return w2_w[:, a, t * P:(t + 1) * P].bitcast(FP8X4)

        def spread(gain):
            return gain.unsqueeze(1).to_broadcast([P, 2 * STRIP, PACK])

        def as_words(tile, pair):
            return tile[:, pair * 2 * BANK:(pair + 1) * 2 * BANK].rearrange("p (n t) -> p n t", t=PACK)

        h_w = keep.tile([P, S], U32, name="h_w", align_bytes=64)
        h_sc = keep.tile([P, S], U8, name="h_sc", align_bytes=64)
        f_w = keep.tile([P, S], U32, name="f_w", align_bytes=64)
        f_sc = keep.tile([P, S], U8, name="f_sc", align_bytes=64)

        def quantise_half(rounded, words, plane, hf):
            cols = slice(hf * BANK, (hf + 1) * BANK)
            nc.vector.quantize_mx(out=words[:, cols].bitcast(FP8X4), scales=plane[:, cols], in_=rounded[:, :])

        strips_a_half = STRIPS // HALVES
        h_rounded = keep.tile([P, HALVES * PACK * BANK], BF16, name="h_rounded", tag="w2_bf2", align_bytes=64)
        for hf in range(HALVES):
            act = ring.tile([P, PACK * BANK], F32, name="act", tag="act", bufs=4)
            for i in range(strips_a_half):
                strip = hf * strips_a_half + i
                bank = h_banks[strip]
                first_stage_pass(bank, strip, 1, w1_slice, w1_sc)
                nc.scalar.activation(act[:, i * BANK:(i + 1) * BANK].rearrange("p (n t) -> p n t", t=PACK),
                                     bank[:].rearrange("p t n -> p n t"), ACT.Tanh)
            rounded = h_rounded[:, hf * PACK * BANK:(hf + 1) * PACK * BANK]
            for pair in range(2):
                nc.vector.tensor_tensor(as_words(rounded, pair), as_words(act, pair), spread(g1), ALU.mult)
            quantise_half(rounded, h_w, h_sc, hf)

        for q in range(QUADS):
            nc.gpsimd.dma_start(tab2_sc[32 * q + V2_ROW:32 * q + V2_ROW + 4, :].bitcast(I32),
                                tab2_scales[0, 4 * q:4 * q + 4, :].bitcast(I32))
        v2_w = keep.tile([P, S2], U32, name="v2_w", align_bytes=64)
        nc.vector.tensor_copy(v2_w[:], tab2_w[:].indirect(idx2[:]))
        v2_sc = keep.tile([P, S2], U8, name="v2_sc", tag="w2_bf1", align_bytes=64)
        nc.vector.tensor_copy(v2_sc[:], tab2_sc[:].indirect(idx2[:]))
        w3_w = keep.tile([P, S2], U32, name="w3_w", tag="w2_bf0", align_bytes=64)
        nc.sync.dma_start(w3_w[:].bitcast(I32), words_of(w3_words[0]))
        w3_sc = keep.tile([P, S2], U8, name="w3_sc", tag="planes", align_bytes=64)
        for q in range(QUADS):
            nc.sync.dma_start(w3_sc[32 * q + W3_ROW:32 * q + W3_ROW + 4, :].bitcast(I32),
                              w3_scales[0, 4 * q:4 * q + 4, :].bitcast(I32))
        fit_sb = shared.tile([P, M_TILES, NP], F32, name="fit_sb", offset=4 * S, align_bytes=64)
        nc.sync.dma_start(fit_sb[:], fit.rearrange("(j p) n -> p j n", p=P))

        for hf in range(HALVES):
            act = ring.tile([P, PACK * BANK], F32, name="act", tag="act", bufs=4)
            for i in range(strips_a_half):
                strip = hf * strips_a_half + i
                bank = next_bank([P, PACK, STRIP])
                for a in range(PASSES):
                    first_stage_pass(bank, strip, a, w2_slice, w2_sc)
                sine = ring.tile([P, BANK], F32, name="sine", tag="sine")
                nc.scalar.activation(sine[:].rearrange("p (n t) -> p n t", t=PACK), bank[:].rearrange("p t n -> p n t"),
                                     ACT.Sin, bias=quarter_pi[:], scale=0.5)
                nc.scalar.activation(act[:, i * BANK:(i + 1) * BANK], sine[:], ACT.Square, scale=math.sqrt(2.0))
            rounded = ring.tile([P, PACK * BANK], BF16, name="rounded", tag="rounded", align_bytes=64)
            for pair in range(2):
                nc.vector.scalar_tensor_tensor(as_words(rounded, pair), as_words(act, pair), 1.0, spread(g2),
                                               ALU.subtract, ALU.mult)
            quantise_half(rounded, f_w, f_sc, hf)

        bias = keep.tile([P, M_TILES], F32, name="bias", tag="column", align_bytes=64)
        with nc.allow_non_contiguous_dma(reason="one margin a partition"):
            nc.sync.dma_start(bias[:], margin.rearrange("(j p) -> p j", p=P))

        def scores(j, stationary, plane, row, words, moving_plane, name, on_vector):
            rows = slice(j * P, (j + 1) * P)
            whole = ring.tile([P, S], F32, name=name, tag=name, bufs=4)
            for hf in range(HALVES):
                cols = slice(hf * BANK, (hf + 1) * BANK)
                bank = next_bank([P, BANK])
                nc.tensor.matmul_mx(out=bank[:], lhsT=stationary[:, rows].bitcast(FP8X4), lhsT_scale=plane[row:P, rows],
                                    rhs=words[:, cols].bitcast(FP8X4), rhs_scale=moving_plane[:, cols],
                                    start=True, stop=True)
                if hf in on_vector:
                    nc.vector.tensor_copy(whole[:, cols], bank[:])
                else:
                    nc.scalar.copy(whole[:, cols], bank[:])
            return whole

        def look(j):
            e_tile = scores(j, v2_w, v2_sc, V2_ROW, h_w, h_sc, "e", E_V[j])
            gate = keep.tile([P, NP], F32, name=f"gate{j}")
            nc.scalar.activation(gate[:], e_tile[:].indirect(p1[:]), ACT.Sigmoid, bias=bias[:, j:j + 1])
            return gate

        gates = [look(j) for j in range(LAG)]
        for j in range(M_TILES):
            d_tile = scores(j, w3_w, w3_sc, W3_ROW, f_w, f_sc, "d", D_V[j])
            if j + LAG < M_TILES:
                gates.append(look(j + LAG))
            gate = gates[j]
            gated = ring.tile([P, NP], F32, name="gated", tag="gated")
            picked = ring.tile([P, NP], F32, name="picked", tag="picked")
            best = keep.tile([P, NP], F32, name=f"best{j}")
            nc.vector.tensor_tensor(gated[:], gate[:], fit_sb[:, j, :], ALU.mult)
            nc.vector.tensor_copy(picked[:], d_tile[:].indirect(p2[:]))
            pieces = 2 if j == M_TILES - 1 else 1
            for i in range(pieces):
                cols = slice(i * NP // pieces, (i + 1) * NP // pieces)
                nc.vector.tensor_tensor(best[:, cols], gated[:, cols], picked[:, cols], ALU.max)
                nc.sync.dma_start(out[j * P:(j + 1) * P, cols], best[:, cols])
